import numpy as np, ml_dtypes
CORES = [2,3,42,43,82,83,122,123]
N = 8
import mx_ref
BF = ml_dtypes.bfloat16
def entries(a):
    return np.ascontiguousarray(a.T).reshape(-1)
def table(e):
    return np.ascontiguousarray(np.reshape(e, (-1, 16)).T).astype(np.int32)
def cols(t, e):
    v = np.concatenate([t.reshape(128, -1, 4), np.zeros((128, 1, 4), BF)], axis=1)
    return np.ascontiguousarray(v[:, e]).reshape(128, -1)
def tile(rs):
    return np.stack(rs, axis=2).reshape(128, -1).astype(BF)
def cut(t, i, w=512):
    return t[:, w * i:w * i + w]
def f(rng, *shape):
    return mx_ref.flush((rng.standard_normal(shape, dtype=np.float32) * np.exp2(rng.integers(-2, 3, shape[:-1] + (1,)))).astype(BF))
def wide(rng, *shape, cols=0):
    v = rng.standard_normal(shape, dtype=np.float32) * np.exp2(rng.integers(-12, 13, shape)).astype(np.float32)
    if cols: v *= np.repeat(np.exp2(rng.integers(-cols, cols + 1, shape[:-2] + (1, shape[-1] // 4))) * (rng.random(shape[:-2] + (1, shape[-1] // 4)) > 0.0625), 4, axis=-1).astype(np.float32)
    return mx_ref.flush(v.astype(BF))
T, CAPA, CAPB, TR = 512, 96, 112, 16
def mix(rng, n, la=0, lb=0):
    n = n.copy()
    for _ in range(4000):
        p, q = rng.integers(0, N, (2, 3)); k = rng.integers(0, 4)
        p2, q2 = p.copy(), q.copy(); m = n.copy()
        if k == 3: p2[1] = q[1]
        else: p2[k], q2[k] = q[k], p[k]
        m[tuple(p)] -= 1; m[tuple(p2)] += 1
        if k < 3: m[tuple(q)] -= 1; m[tuple(q2)] += 1
        sa, ab = m.sum(axis=2), m.sum(axis=0)
        if m.min() >= 0 and m.max() <= TR and (sa <= CAPA).all() and (sa >= la).all() and (ab <= CAPB).all() and (ab >= lb).all(): n = m
    return n
def even():
    return np.full((N, N, N), T // N ** 2)
def places(rng, k, cap, by=None):
    out = np.zeros(len(k), int)
    for g in np.unique(k):
        j = np.flatnonzero(k == g)
        if by is None: out[j] = g * cap + rng.permutation(cap)[:len(j)]
        else: out[j[np.argsort(by[j])]] = g * cap + cap - 1 - np.arange(len(j))
    return out
def lists(rng, n, back=False):
    s, a, b = np.repeat(np.argwhere(n >= 0), n.reshape(-1), axis=0).T
    col = np.concatenate([rng.permutation(T) for r in range(N)])
    snd, pas, tri = np.full(N * N * CAPA, -1), np.full(N * N * CAPB, -1), np.full(N * N * N * TR, -1)
    p1 = places(rng, s * N + a, CAPA, col if back else None); snd[p1] = col
    arr = s * CAPA + p1 % CAPA
    p2 = places(rng, a * N + b, CAPB, arr if back else None); pas[p2] = arr
    p3 = places(rng, (s * N + a) * N + b, TR, col if back else None); tri[p3] = col
    c, t = a * CAPB + p2 % CAPB, (s * N + a) * TR + p3 % TR
    plc, plt = [], []
    for r in range(N):
        j = rng.permutation(np.flatnonzero(b == r))
        if back: j = j[np.argsort(-c[j])]
        plc.append(table(c[j])); plt.append(table(t[j]))
    return {"snd": np.stack([table(v) for v in snd.reshape(N, -1)]), "pas": np.stack([table(v) for v in pas.reshape(N, -1)]), "tri": np.stack([table(v) for v in tri.reshape(N, -1)]), "plc": np.stack(plc), "plt": np.stack(plt)}
def values(rng):
    return {"x": f(rng, N, 128, 4 * T), "w": f(rng, N, 128, 2048), "vv": f(rng, N, 128, 512)}
def setup_inputs(rng):
    return {**values(rng), **lists(rng, mix(rng, even()))}
def heavy(rng, d):
    n = even()
    for k in range(CAPB // N - T // N ** 2):
        for s in range(N):
            for a in range(N):
                n[s, a, (a + d) % N] += 1; n[s, a, (a + d + 1 + (s + k) % (N - 1)) % N] -= 1
    return {**values(rng), **lists(rng, mix(rng, n, lb=CAPB * np.roll(np.eye(N, dtype=int), d, axis=1)))}
def setup_inputs_diag(rng):
    return heavy(rng, 0)
def setup_inputs_onward(rng):
    return heavy(rng, int(rng.integers(1, N)))
def setup_inputs_full(rng):
    k = T // CAPA
    g = np.zeros((N, N), int); g[:, :k] = CAPA; g[:, k] = T - k * CAPA
    g = np.stack([np.roll(g[s], s) for s in range(N)])[rng.permutation(N)][:, rng.permutation(N)]
    return {**values(rng), **lists(rng, mix(rng, np.repeat(g[:, :, None] // N, N, axis=2), la=np.where(g == CAPA, CAPA, 0)))}
def setup_inputs_reversed(rng):
    return {**values(rng), **lists(rng, mix(rng, even()), back=True)}
def setup_inputs_spread(rng):
    d = setup_inputs(rng); d["x"] = wide(rng, N, 128, 4 * T); return d
def check_inputs(d):
    b = []
    snd, pas, tri, plc, plt = [[entries(d[k][r]) for r in range(N)] for k in ("snd", "pas", "tri", "plc", "plt")]
    for r in range(N):
        if snd[r].min() < -1 or not np.array_equal(np.sort(snd[r][snd[r] >= 0]), np.arange(T)): b.append("snd")
        if tri[r].min() < -1 or not np.array_equal(np.sort(tri[r][tri[r] >= 0]), np.arange(T)): b.append("tri")
        for a in range(N):
            u, v = snd[r][a * CAPA:(a + 1) * CAPA], tri[r][a * N * TR:(a + 1) * N * TR]
            if not np.array_equal(np.sort(u[u >= 0]), np.sort(v[v >= 0])): b.append("tri")
    arrived = [np.concatenate([snd[s][a * CAPA:(a + 1) * CAPA] for s in range(N)]) for a in range(N)]
    for a in range(N):
        if pas[a].min() < -1 or not np.array_equal(np.sort(pas[a][pas[a] >= 0]), np.flatnonzero(arrived[a] >= 0)): b.append("pas")
    if b: return b
    for r in range(N):
        k = np.concatenate([pas[a][r * CAPB:(r + 1) * CAPB] for a in range(N)])
        t = np.concatenate([tri[s][(a * N + r) * TR:(a * N + r + 1) * TR] for s in range(N) for a in range(N)])
        if not np.array_equal(np.sort(plc[r]), np.flatnonzero(k >= 0)): b.append("plc"); continue
        if not np.array_equal(np.sort(plt[r]), np.flatnonzero(t >= 0)): b.append("plt"); continue
        a, m = plc[r] // CAPB, k[plc[r]]
        if (plt[r] // TR != m // CAPA * N + a).any() or (t[plt[r]] != np.stack(arrived)[a, m]).any(): b.append("plt")
    return b
def reference(x, w, vv, snd, pas, tri, plc, plt):
    h = []
    for a in range(N):
        q = mx_ref.quantize(np.concatenate([cols(x[s], entries(snd[s])[a * CAPA:(a + 1) * CAPA]) for s in range(N)], axis=1))
        h.append(tile([np.maximum(mx_ref.matmul(mx_ref.quantize(cut(w[a], i)), q), np.float32(0)) * np.float32(0.043) for i in range(4)]))
    y = np.zeros((N, 128, T), np.float32)
    for b in range(N):
        t = np.concatenate([cols(h[a], entries(pas[a])[b * CAPB:(b + 1) * CAPB]) for a in range(N)], axis=1)
        y[b] = mx_ref.matmul(mx_ref.quantize(vv[b]), mx_ref.quantize(cols(t, entries(plc[b]))))
    return {"y": y}

@@ -1,0 +1,210 @@
+from concourse.bass import DstId, RemoteDMATransfer
+from concourse.mybir import AluOpType, ActivationFunctionType, dt
+
+N, TOK, TR = 8, 512, 16
+B = N * TR
+ALL = N * B
+
+SCRATCH = {
+    "trib": ("sbuf", [128, ALL // 16], "int32"),
+    "off1": ("sbuf", [128, ALL // 16], "uint16"),
+    "pltb": ("sbuf", [128, TOK // 16], "int32"),
+    "pa": ("sbuf", [128, TOK // 16], "int32"),
+    "pb": ("sbuf", [128, TOK // 16], "int32"),
+    "pc": ("sbuf", [128, TOK // 16], "int32"),
+    "pd": ("sbuf", [128, TOK // 16], "int32"),
+    "off2": ("sbuf", [128, TOK // 16], "uint16"),
+    "xb": ("sbuf", [128, 4 * TOK], "bfloat16"),
+    "wb": ("sbuf", [128, 2048], "bfloat16"),
+    "vb": ("sbuf", [128, 512], "bfloat16"),
+    "xg": ("sbuf", [128, 4 * ALL], "bfloat16"),
+    "h": ("sbuf", [128, 4 * ALL], "bfloat16"),
+    "wq": ("sbuf", [128, 512], "float8_e4m3fn_x4"),
+    "ws": ("sbuf", [128, 512], "uint8"),
+    "vq": ("sbuf", [128, 128], "float8_e4m3fn_x4"),
+    "vs": ("sbuf", [128, 128], "uint8"),
+    "xq": ("sbuf", [128, ALL], "float8_e4m3fn_x4"),
+    "xs": ("sbuf", [128, ALL], "uint8"),
+    "hq": ("sbuf", [128, ALL], "float8_e4m3fn_x4"),
+    "hs": ("sbuf", [128, ALL], "uint8"),
+    "aq": ("sbuf", [128, ALL], "float8_e4m3fn_x4"),
+    "as_": ("sbuf", [128, ALL], "uint8"),
+    "bq": ("sbuf", [128, ALL], "float8_e4m3fn_x4"),
+    "bs": ("sbuf", [128, ALL], "uint8"),
+    "yv": ("sbuf", [128, ALL], "float32"),
+    "yt": ("sbuf", [128, TOK], "float32"),
+    "ps": ("psum", [128, 4096], "float32"),
+}
+SEMAPHORES = (["ld_tri", "ld_x", "ld_w", "ld_v", "ld_plt", "off1r", "off2r", "wqr", "vqr", "pt1", "pt2", "pt3",
+               "ls", "fc", "yv0", "yv1", "st0", "st1"]
+              + ["gx%d" % p for p in range(4)] + ["q1_%d" % p for p in range(4)] + ["q2_%d" % p for p in range(4)]
+              + ["in1_%d" % r for r in range(N)] + ["in2_%d" % r for r in range(N)]
+              + ["ma%d" % k for k in range(N)] + ["mb%d" % k for k in range(N)] + ["rl%d" % k for k in range(N)]
+              + ["fm%d" % k for k in range(N)])
+
+
+def bits(engines):
+    return sum(1 << e for e in engines)
+
+
+def rank_program(g, core, T, topo):
+    rank = T.rank_of(core)
+    if rank is None:
+        return
+    S = T.sem
+    A = AluOpType
+    F = ActivationFunctionType
+    chips = []
+    for c in T.cores:
+        if topo.chip(c) not in chips:
+            chips.append(topo.chip(c))
+    groups = [[r for r in range(N) if topo.chip(T.cores[r]) == c] for c in chips]
+    me = chips.index(topo.chip(core))
+    G = len(groups)
+    out_order = [(me + d) % G for d in range(1, G)]
+    in_order = [(me - d) % G for d in range(1, G)]
+    sib = [r for r in groups[me] if r != rank]
+    PC = B * len(groups[0])
+    far = topo.engines(core, T.cores[groups[out_order[0]][0]])
+    near = [e for e in topo.engines(core, T.cores[sib[0]]) if e not in far][:len(far) // 2]
+
+    def blk(r):
+        return slice(B * r, B * (r + 1))
+
+    def transfers(q, code, dst_ranks, src, dst, sem):
+        out = []
+        for r, eng in dst_ranks:
+            rid, pid, _ = topo.addr(T.cores[r])
+            a, b = src[:, blk(r)], dst[:, blk(rank)]
+            if code:
+                a, b = a.bitcast(dt.uint8), b.bitcast(dt.uint8)
+            out.append(RemoteDMATransfer(dst_ids=[DstId(rid=rid, pnc=pid)], dma_engine_mask=bits(eng),
+                                         remote_sem=S["%s_%d" % (sem, rank)], src=a, dst=b))
+        q.remote_dma_fused(out, local_sem=S["ls"])
+
+    def chip_engines(gi):
+        n = len(far) // len(groups[gi])
+        return [(r, far[n * i:n * (i + 1)]) for i, r in enumerate(groups[gi])]
+
+    for k in range(8):
+        q = g.sync if k < 3 else g.scalar
+        q.dma_start(T.trib[16 * k:16 * k + 16, :], T.tri[:]).then_inc(S["ld_tri"], 16)
+    g.sync.dma_start(T.xb[:], T.x[:]).then_inc(S["ld_x"], 16)
+    g.sync.wait_ge(S["ld_x"], 16)
+    g.sync.dma_start(T.wb[:], T.w[:]).then_inc(S["ld_w"], 16)
+    g.sync.dma_start(T.vb[:], T.vv[:]).then_inc(S["ld_v"], 16)
+    for k in range(8):
+        g.sync.dma_start(T.pltb[16 * k:16 * k + 16, :], T.plt[:]).then_inc(S["ld_plt"], 16)
+
+    V = g.vector
+    V.wait_ge(S["ld_tri"], 128)
+    V.tensor_scalar(T.off1[:], T.trib[:], 4.0, 0.0, A.mult, A.max).then_inc(S["off1r"], 1)
+    V.wait_ge(S["off1r"], 1)
+    V.wait_ge(S["ld_x"], 16)
+    g.scalar.wait_ge(S["off1r"], 1)
+    g.scalar.wait_ge(S["ld_x"], 16)
+    own = G - 1
+    for p, gi in enumerate(out_order + [me]):
+        c0 = PC * gi
+        off = T.off1[:, c0 // 16:(c0 + PC) // 16]
+        ns = 3 if p == own else 2
+        for t in range(4):
+            o = T.xg[:, 4 * c0 + t:4 * (c0 + PC):4]
+            i = T.xb[:, t:4 * TOK].indirect(off)
+            if t < ns:
+                g.scalar.activation(o, i, F.Copy).then_inc(S["gx%d" % p], 1)
+            else:
+                V.tensor_copy(o, i).then_inc(S["gx%d" % p], 1)
+        V.wait_ge(S["gx%d" % p], 4)
+        V.quantize_mx(T.xq[:, c0:c0 + PC], T.xs[:, c0:c0 + PC], T.xg[:, 4 * c0:4 * (c0 + PC)]).then_inc(S["q1_%d" % p], 1)
+        g.wait_ge(S["q1_%d" % p], 1)
+        dst = chip_engines(gi) if p < own else [(sib[0], near)]
+        transfers(g, True, dst, T.xq, T.aq, "in1")
+        transfers(g, False, dst, T.xs, T.as_, "in1")
+
+    V.wait_ge(S["ld_w"], 16)
+    V.quantize_mx(T.wq[:], T.ws[:], T.wb[:]).then_inc(S["wqr"], 1)
+    V.wait_ge(S["ld_v"], 16)
+    V.quantize_mx(T.vq[:], T.vs[:], T.vb[:]).then_inc(S["vqr"], 1)
+    V.wait_ge(S["ld_plt"], 128)
+    V.tensor_scalar(T.pa[:], T.pltb[:], B - 1, None, A.bitwise_and).then_inc(S["pt1"], 1)
+    V.tensor_scalar(T.pb[:], T.pltb[:], B.bit_length() - 1, None, A.logical_shift_right).then_inc(S["pt1"], 1)
+    V.wait_ge(S["pt1"], 2)
+    V.tensor_scalar(T.pc[:], T.pa[:], float(N), None, A.mult).then_inc(S["pt2"], 1)
+    V.wait_ge(S["pt2"], 1)
+    V.tensor_tensor(T.pd[:], T.pc[:], T.pb[:], A.add).then_inc(S["pt3"], 1)
+    V.wait_ge(S["pt3"], 1)
+    V.tensor_copy(T.off2[:], T.pd[:]).then_inc(S["off2r"], 1)
+
+    order = [rank] + groups[in_order[0]] + groups[in_order[1]] + sib + groups[in_order[2]]
+    E = g.tensor
+    E.wait_ge(S["wqr"], 1)
+    for k, s in enumerate(order):
+        if s == rank:
+            E.wait_ge(S["q1_%d" % own], 1)
+            q, sc = T.xq, T.xs
+        else:
+            E.wait_ge(S["in1_%d" % s], 2 * len(near))
+            q, sc = T.aq, T.as_
+        if k >= 2:
+            E.wait_ge(S["rl%d" % (k - 2)], 4)
+        base = 2048 * (k % 2)
+        for i in (0, 2, 1, 3):
+            sem = S[("ma%d" if i < 2 else "mb%d") % k]
+            E.matmul_mx(T.ps[:, base + 512 * i:base + 512 * i + B], T.wq[:, 128 * i:128 * i + 128],
+                        T.ws[:, 128 * i:128 * i + 128], q[:, blk(s)], sc[:, blk(s)], True, True).then_inc(sem, 1)
+        g.scalar.wait_ge(S["ma%d" % k], 2)
+        V.wait_ge(S["mb%d" % k], 2)
+        for i in range(4):
+            o = T.h[:, 4 * s + i:4 * ALL:4 * N]
+            z = T.ps[:, base + 512 * i:base + 512 * i + B]
+            if i < 2:
+                g.scalar.activation(o, z, F.Relu, scale=0.043).then_inc(S["rl%d" % k], 1)
+            else:
+                V.tensor_scalar(o, z, 0.0, 0.043, A.max, A.mult).then_inc(S["rl%d" % k], 1)
+    for k in range(N):
+        V.wait_ge(S["rl%d" % k], 4)
+    for p, gi in enumerate(out_order + [me]):
+        c0 = PC * gi
+        V.quantize_mx(T.hq[:, c0:c0 + PC], T.hs[:, c0:c0 + PC], T.h[:, 4 * c0:4 * (c0 + PC)]).then_inc(S["q2_%d" % p], 1)
+    for p, gi in enumerate(out_order):
+        g.wait_ge(S["q2_%d" % p], 1)
+        dst = chip_engines(gi)
+        if p == own - 1:
+            g.wait_ge(S["q2_%d" % own], 1)
+            dst = dst + [(sib[0], near)]
+        transfers(g, True, dst, T.hq, T.bq, "in2")
+        transfers(g, False, dst, T.hs, T.bs, "in2")
+
+    E.wait_ge(S["vqr"], 1)
+    E.wait_ge(S["rl%d" % (N - 2)], 4)
+    E.wait_ge(S["rl%d" % (N - 1)], 4)
+    for m, a in enumerate(order):
+        if a == rank:
+            E.wait_ge(S["q2_%d" % own], 1)
+            q, sc = T.hq, T.hs
+        else:
+            E.wait_ge(S["in2_%d" % a], 2 * len(near))
+            q, sc = T.bq, T.bs
+        z = T.ps[:, 512 * m:512 * m + B]
+        E.matmul_mx(z, T.vq[:], T.vs[:], q[:, blk(a)], sc[:, blk(a)], True, True).then_inc(S["fm%d" % m], 1)
+        if m % 2 == 0:
+            g.scalar.wait_ge(S["fm%d" % m], 1)
+            g.scalar.activation(T.yv[:, blk(a)], z, F.Copy).then_inc(S["fc"], 1)
+        else:
+            V.wait_ge(S["fm%d" % m], 1)
+            V.tensor_copy(T.yv[:, blk(a)], z).then_inc(S["fc"], 1)
+    H = TOK // 2
+    g.scalar.wait_ge(S["off2r"], 1)
+    g.scalar.wait_ge(S["fc"], N)
+    g.scalar.activation(T.yt[:, 0:H], T.yv[:].indirect(T.off2[:, 0:H // 16]), F.Copy).then_inc(S["yv0"], 1)
+    V.wait_ge(S["off2r"], 1)
+    V.wait_ge(S["fc"], N)
+    V.tensor_copy(T.yt[:, H:TOK], T.yv[:].indirect(T.off2[:, H // 16:TOK // 16])).then_inc(S["yv1"], 1)
+    g.scalar.wait_ge(S["yv0"], 1)
+    g.scalar.dma_start(T.y[:, 0:H], T.yt[:, 0:H]).then_inc(S["st0"], 16)
+    g.sync.wait_ge(S["yv1"], 1)
+    g.sync.dma_start(T.y[:, H:TOK], T.yt[:, H:TOK]).then_inc(S["st1"], 16)
+    g.scalar.wait_ge(S["st0"], 16)
+    g.sync.wait_ge(S["st1"], 16)
+    g.wait_ge(S["ls"], 2 * ((G - 1) * 2 * len(far) + 2 * len(near)))

@@ -4,56 +4,72 @@ from concourse.mybir import AluOpType, ActivationFunctionType, dt
 N, TOK, TR = 8, 512, 16
 B = N * TR
 ALL = N * B
+HB = B // 2
+HA = ALL // 2
 
 SCRATCH = {
     "trib": ("sbuf", [128, ALL // 16], "int32"),
     "off1": ("sbuf", [128, ALL // 16], "uint16"),
     "pltb": ("sbuf", [128, TOK // 16], "int32"),
-    "pa": ("sbuf", [128, TOK // 16], "int32"),
-    "pb": ("sbuf", [128, TOK // 16], "int32"),
-    "pc": ("sbuf", [128, TOK // 16], "int32"),
-    "pd": ("sbuf", [128, TOK // 16], "int32"),
     "off2": ("sbuf", [128, TOK // 16], "uint16"),
     "xb": ("sbuf", [128, 4 * TOK], "bfloat16"),
     "wb": ("sbuf", [128, 2048], "bfloat16"),
     "vb": ("sbuf", [128, 512], "bfloat16"),
     "xg": ("sbuf", [128, 4 * ALL], "bfloat16"),
-    "h": ("sbuf", [128, 4 * ALL], "bfloat16"),
     "wq": ("sbuf", [128, 512], "float8_e4m3fn_x4"),
     "ws": ("sbuf", [128, 512], "uint8"),
     "vq": ("sbuf", [128, 128], "float8_e4m3fn_x4"),
     "vs": ("sbuf", [128, 128], "uint8"),
     "xq": ("sbuf", [128, ALL], "float8_e4m3fn_x4"),
     "xs": ("sbuf", [128, ALL], "uint8"),
-    "hq": ("sbuf", [128, ALL], "float8_e4m3fn_x4"),
-    "hs": ("sbuf", [128, ALL], "uint8"),
     "aq": ("sbuf", [128, ALL], "float8_e4m3fn_x4"),
     "as_": ("sbuf", [128, ALL], "uint8"),
-    "bq": ("sbuf", [128, ALL], "float8_e4m3fn_x4"),
-    "bs": ("sbuf", [128, ALL], "uint8"),
+    "rq": ("sbuf", [128, B], "float8_e4m3fn_x4"),
+    "rs": ("sbuf", [128, B], "uint8"),
     "yv": ("sbuf", [128, ALL], "float32"),
     "yt": ("sbuf", [128, TOK], "float32"),
     "ps": ("psum", [128, 4096], "float32"),
 }
-SEMAPHORES = (["ld_tri", "ld_x", "ld_w", "ld_v", "ld_plt", "off1r", "off2r", "wqr", "vqr", "pt1", "pt2", "pt3",
-               "ls", "fc", "yv0", "yv1", "st0", "st1"]
-              + ["gx%d" % p for p in range(4)] + ["q1_%d" % p for p in range(4)] + ["q2_%d" % p for p in range(4)]
-              + ["in1_%d" % r for r in range(N)] + ["in2_%d" % r for r in range(N)]
+for _f in range(2):
+    SCRATCH["h%d" % _f] = ("sbuf", [128, 4 * HA], "bfloat16")
+    SCRATCH["hq%d" % _f] = ("sbuf", [128, HA], "float8_e4m3fn_x4")
+    SCRATCH["hs%d" % _f] = ("sbuf", [128, HA], "uint8")
+    SCRATCH["bq%d" % _f] = ("sbuf", [128, 7 * HB], "float8_e4m3fn_x4")
+    SCRATCH["bs%d" % _f] = ("sbuf", [128, 7 * HB], "uint8")
+for _f in range(10):
+    SCRATCH["n%d" % _f] = ("sbuf", [128, TOK // 16], "int32")
+SEMAPHORES = (["ld_tri", "ld_x", "ld_w", "ld_v", "ld_plt", "off1r", "off2r", "wqr", "vqr", "pt",
+               "ls", "fc", "fcs", "yv0", "yv1", "st0", "st1", "viaq", "vias"]
+              + ["gx%d" % p for p in range(4)] + ["q1_%d" % p for p in range(4)]
+              + ["q2%d_%d" % (f, p) for p in range(4) for f in range(2)]
+              + ["in1_%d" % r for r in range(N)] + ["in2%d_%d" % (f, r) for r in range(N) for f in range(2)]
               + ["ma%d" % k for k in range(N)] + ["mb%d" % k for k in range(N)] + ["rl%d" % k for k in range(N)]
-              + ["fm%d" % k for k in range(N)])
+              + ["fm%d" % k for k in range(9)])
 
 
 def bits(engines):
     return sum(1 << e for e in engines)
 
 
+def via(r, T, topo):
+    c = T.cores[r]
+    free = [o for o in topo.cores_of(c) if topo.die(o) != topo.die(c) and T.rank_of(o) is None
+            and all(topo.may_write(o, d) for d in T.cores if topo.chip(d) != topo.chip(c))]
+    return free[[d for d in T.cores if topo.chip(d) == topo.chip(c)].index(c)]
+
+
 def rank_program(g, core, T, topo):
     rank = T.rank_of(core)
-    if rank is None:
-        return
+    hands_on = rank is None
+    if hands_on:
+        served = [r for r in range(N) if via(r, T, topo) == core]
+        if not served:
+            return
+        rank = served[0]
     S = T.sem
     A = AluOpType
     F = ActivationFunctionType
+    V, E, C = g.vector, g.tensor, g.scalar
     chips = []
     for c in T.cores:
         if topo.chip(c) not in chips:
@@ -63,31 +79,47 @@ def rank_program(g, core, T, topo):
     G = len(groups)
     out_order = [(me + d) % G for d in range(1, G)]
     in_order = [(me - d) % G for d in range(1, G)]
-    sib = [r for r in groups[me] if r != rank]
-    PC = B * len(groups[0])
+    sib = [r for r in groups[me] if r != rank][0]
+    PC = 2 * B
     far = topo.engines(core, T.cores[groups[out_order[0]][0]])
-    near = [e for e in topo.engines(core, T.cores[sib[0]]) if e not in far][:len(far) // 2]
+    near = [e for e in topo.engines(core, T.cores[sib]) if e not in far][:len(far) // 2]
+    n = len(far) // 2
 
-    def blk(r):
-        return slice(B * r, B * (r + 1))
+    def share(ranks):
+        k = len(far) // len(ranks)
+        return [(r, far[k * i:k * (i + 1)]) for i, r in enumerate(ranks)]
 
-    def transfers(q, code, dst_ranks, src, dst, sem):
+    def slot(b, a):
+        d = (b // 2 - a // 2) % G
+        return 6 if d == 0 else 2 * (d - 1) + a % 2
+
+    def views(src, dst, lo, to, w, code):
+        a, b = src[:, lo:lo + w], dst[:, to:to + w]
+        return (a.bitcast(dt.uint8), b.bitcast(dt.uint8)) if code else (a, b)
+
+    def send(dsts, src, dst, place, sem, code):
         out = []
-        for r, eng in dst_ranks:
+        for r, eng in dsts:
             rid, pid, _ = topo.addr(T.cores[r])
-            a, b = src[:, blk(r)], dst[:, blk(rank)]
-            if code:
-                a, b = a.bitcast(dt.uint8), b.bitcast(dt.uint8)
+            a, b = views(src, dst, *place(r), code)
             out.append(RemoteDMATransfer(dst_ids=[DstId(rid=rid, pnc=pid)], dma_engine_mask=bits(eng),
                                          remote_sem=S["%s_%d" % (sem, rank)], src=a, dst=b))
-        q.remote_dma_fused(out, local_sem=S["ls"])
+        g.remote_dma_fused(out, local_sem=S["ls"])
 
-    def chip_engines(gi):
-        n = len(far) // len(groups[gi])
-        return [(r, far[n * i:n * (i + 1)]) for i, r in enumerate(groups[gi])]
+    last = out_order[G - 2]
+    if hands_on:
+        def place_on(r):
+            return HB * groups[last].index(r), HB * slot(r, rank), HB
+
+        g.wait_ge(S["viaq"], len(near))
+        send(share(groups[last]), T.rq, T.bq0, place_on, "in20", True)
+        g.wait_ge(S["vias"], len(near))
+        send(share(groups[last]), T.rs, T.bs0, place_on, "in20", False)
+        g.wait_ge(S["ls"], 2 * len(far))
+        return
 
     for k in range(8):
-        q = g.sync if k < 3 else g.scalar
+        q = g.sync if k < 3 else C
         q.dma_start(T.trib[16 * k:16 * k + 16, :], T.tri[:]).then_inc(S["ld_tri"], 16)
     g.sync.dma_start(T.xb[:], T.x[:]).then_inc(S["ld_x"], 16)
     g.sync.wait_ge(S["ld_x"], 16)
@@ -96,115 +128,185 @@ def rank_program(g, core, T, topo):
     for k in range(8):
         g.sync.dma_start(T.pltb[16 * k:16 * k + 16, :], T.plt[:]).then_inc(S["ld_plt"], 16)
 
-    V = g.vector
     V.wait_ge(S["ld_tri"], 128)
     V.tensor_scalar(T.off1[:], T.trib[:], 4.0, 0.0, A.mult, A.max).then_inc(S["off1r"], 1)
     V.wait_ge(S["off1r"], 1)
     V.wait_ge(S["ld_x"], 16)
-    g.scalar.wait_ge(S["off1r"], 1)
-    g.scalar.wait_ge(S["ld_x"], 16)
-    own = G - 1
-    for p, gi in enumerate(out_order + [me]):
+    C.wait_ge(S["off1r"], 1)
+    C.wait_ge(S["ld_x"], 16)
+
+    def place1(r):
+        return B * r, B * rank, B
+
+    for p, gi in enumerate([out_order[0], me, out_order[1], out_order[2]]):
         c0 = PC * gi
         off = T.off1[:, c0 // 16:(c0 + PC) // 16]
-        ns = 3 if p == own else 2
+        ns = 3 if gi == me else 2
         for t in range(4):
             o = T.xg[:, 4 * c0 + t:4 * (c0 + PC):4]
             i = T.xb[:, t:4 * TOK].indirect(off)
             if t < ns:
-                g.scalar.activation(o, i, F.Copy).then_inc(S["gx%d" % p], 1)
+                C.activation(o, i, F.Copy).then_inc(S["gx%d" % p], 1)
             else:
                 V.tensor_copy(o, i).then_inc(S["gx%d" % p], 1)
         V.wait_ge(S["gx%d" % p], 4)
         V.quantize_mx(T.xq[:, c0:c0 + PC], T.xs[:, c0:c0 + PC], T.xg[:, 4 * c0:4 * (c0 + PC)]).then_inc(S["q1_%d" % p], 1)
+        if gi == me:
+            continue
+        if p == 2:
+            g.wait_ge(S["q1_1"], 1)
         g.wait_ge(S["q1_%d" % p], 1)
-        dst = chip_engines(gi) if p < own else [(sib[0], near)]
-        transfers(g, True, dst, T.xq, T.aq, "in1")
-        transfers(g, False, dst, T.xs, T.as_, "in1")
+        dst = share(groups[gi]) + ([(sib, near)] if p == 2 else [])
+        send(dst, T.xq, T.aq, place1, "in1", True)
+        send(dst, T.xs, T.as_, place1, "in1", False)
 
     V.wait_ge(S["ld_w"], 16)
     V.quantize_mx(T.wq[:], T.ws[:], T.wb[:]).then_inc(S["wqr"], 1)
     V.wait_ge(S["ld_v"], 16)
     V.quantize_mx(T.vq[:], T.vs[:], T.vb[:]).then_inc(S["vqr"], 1)
-    V.wait_ge(S["ld_plt"], 128)
-    V.tensor_scalar(T.pa[:], T.pltb[:], B - 1, None, A.bitwise_and).then_inc(S["pt1"], 1)
-    V.tensor_scalar(T.pb[:], T.pltb[:], B.bit_length() - 1, None, A.logical_shift_right).then_inc(S["pt1"], 1)
-    V.wait_ge(S["pt1"], 2)
-    V.tensor_scalar(T.pc[:], T.pa[:], float(N), None, A.mult).then_inc(S["pt2"], 1)
-    V.wait_ge(S["pt2"], 1)
-    V.tensor_tensor(T.pd[:], T.pc[:], T.pb[:], A.add).then_inc(S["pt3"], 1)
-    V.wait_ge(S["pt3"], 1)
-    V.tensor_copy(T.off2[:], T.pd[:]).then_inc(S["off2r"], 1)
 
-    order = [rank] + groups[in_order[0]] + groups[in_order[1]] + sib + groups[in_order[2]]
-    E = g.tensor
     E.wait_ge(S["wqr"], 1)
-    for k, s in enumerate(order):
-        if s == rank:
-            E.wait_ge(S["q1_%d" % own], 1)
-            q, sc = T.xq, T.xs
-        else:
-            E.wait_ge(S["in1_%d" % s], 2 * len(near))
-            q, sc = T.aq, T.as_
-        if k >= 2:
-            E.wait_ge(S["rl%d" % (k - 2)], 4)
-        base = 2048 * (k % 2)
-        for i in (0, 2, 1, 3):
-            sem = S[("ma%d" if i < 2 else "mb%d") % k]
-            E.matmul_mx(T.ps[:, base + 512 * i:base + 512 * i + B], T.wq[:, 128 * i:128 * i + 128],
-                        T.ws[:, 128 * i:128 * i + 128], q[:, blk(s)], sc[:, blk(s)], True, True).then_inc(sem, 1)
-        g.scalar.wait_ge(S["ma%d" % k], 2)
-        V.wait_ge(S["mb%d" % k], 2)
-        for i in range(4):
-            o = T.h[:, 4 * s + i:4 * ALL:4 * N]
-            z = T.ps[:, base + 512 * i:base + 512 * i + B]
-            if i < 2:
-                g.scalar.activation(o, z, F.Relu, scale=0.043).then_inc(S["rl%d" % k], 1)
+    halves = [[rank] + groups[in_order[0]] + [sib], groups[in_order[1]] + groups[in_order[2]]]
+    k = 0
+    for f, half in enumerate(halves):
+        h, hq, hs = T["h%d" % f], T["hq%d" % f], T["hs%d" % f]
+        for s in half:
+            if s == rank:
+                E.wait_ge(S["q1_1"], 1)
+                q, sc = T.xq, T.xs
             else:
-                V.tensor_scalar(o, z, 0.0, 0.043, A.max, A.mult).then_inc(S["rl%d" % k], 1)
-    for k in range(N):
-        V.wait_ge(S["rl%d" % k], 4)
-    for p, gi in enumerate(out_order + [me]):
-        c0 = PC * gi
-        V.quantize_mx(T.hq[:, c0:c0 + PC], T.hs[:, c0:c0 + PC], T.h[:, 4 * c0:4 * (c0 + PC)]).then_inc(S["q2_%d" % p], 1)
-    for p, gi in enumerate(out_order):
-        g.wait_ge(S["q2_%d" % p], 1)
-        dst = chip_engines(gi)
-        if p == own - 1:
-            g.wait_ge(S["q2_%d" % own], 1)
-            dst = dst + [(sib[0], near)]
-        transfers(g, True, dst, T.hq, T.bq, "in2")
-        transfers(g, False, dst, T.hs, T.bs, "in2")
+                E.wait_ge(S["in1_%d" % s], 2 * n)
+                q, sc = T.aq, T.as_
+            if k >= 2:
+                E.wait_ge(S["rl%d" % (k - 2)], 4)
+            base = 2048 * (k % 2)
+            for i in (0, 2, 1, 3):
+                sem = S[("ma%d" if i < 2 else "mb%d") % k]
+                E.matmul_mx(T.ps[:, base + 512 * i:base + 512 * i + B], T.wq[:, 128 * i:128 * i + 128],
+                            T.ws[:, 128 * i:128 * i + 128], q[:, B * s:B * s + B], sc[:, B * s:B * s + B],
+                            True, True).then_inc(sem, 1)
+            C.wait_ge(S["ma%d" % k], 2)
+            V.wait_ge(S["mb%d" % k], 2)
+            place = 2 * ((me - s // 2) % G % 2) + s % 2
+            for i in range(4):
+                o = h[:, 4 * place + i:4 * HA:16]
+                z = T.ps[:, base + 512 * i:base + 512 * i + B]
+                if i < 2:
+                    C.activation(o, z, F.Relu, scale=0.043).then_inc(S["rl%d" % k], 1)
+                else:
+                    V.tensor_scalar(o, z, 0.0, 0.043, A.max, A.mult).then_inc(S["rl%d" % k], 1)
+            k += 1
+        for j in range(k - 4, k):
+            V.wait_ge(S["rl%d" % j], 4)
+        by = out_order + [me]
+        for p in ((2, 0, 1, 3) if f == 0 else (0, 1, 2, 3)):
+            c0 = B * by[p]
+            V.quantize_mx(hq[:, c0:c0 + B], hs[:, c0:c0 + B], h[:, 4 * c0:4 * (c0 + B)]).then_inc(S["q2%d_%d" % (f, p)], 1)
+
+        def place2(r):
+            return HB * r, HB * slot(r, rank), HB
+
+        if f == 0:
+            g.wait_ge(S["q20_2"], 1)
+            rid, pid, _ = topo.addr(via(rank, T, topo))
+            for src, dst, code, sem in ((hq, T.rq, True, "viaq"), (hs, T.rs, False, "vias")):
+                a, b = views(src, dst, B * last, 0, B, code)
+                g.remote_dma_fused([RemoteDMATransfer(dst_ids=[DstId(rid=rid, pnc=pid)], dma_engine_mask=bits(near),
+                                                      remote_sem=S[sem], src=a, dst=b)], local_sem=S["ls"])
+            calls = ((0, 1, 3),)
+        else:
+            calls = ((0, 1), (2, 3))
+        for ps in calls:
+            for p in ps:
+                g.wait_ge(S["q2%d_%d" % (f, p)], 1)
+            dst = share([r for p in ps if p < G - 1 for r in groups[by[p]]]) + ([(sib, near)] if 3 in ps else [])
+            send(dst, hq, T["bq%d" % f], place2, "in2%d" % f, True)
+            send(dst, hs, T["bs%d" % f], place2, "in2%d" % f, False)
+
+    cnt = [0]
+
+    def num(call, *args):
+        call(*args).then_inc(S["pt"], 1)
+        cnt[0] += 1
+
+    def done():
+        V.wait_ge(S["pt"], cnt[0])
+
+    t = [T["n%d" % i][:] for i in range(10)]
+    V.wait_ge(S["ld_plt"], 128)
+    num(V.tensor_scalar, t[0], T.pltb[:], 127, None, A.bitwise_and)
+    num(V.tensor_scalar, t[1], T.pltb[:], 5, 3, A.logical_shift_right, A.bitwise_and)
+    num(V.tensor_scalar, t[2], T.pltb[:], 8, None, A.logical_shift_right)
+    num(V.tensor_scalar, t[3], T.pltb[:], 7, 1, A.logical_shift_right, A.bitwise_and)
+    done()
+    num(V.tensor_tensor, t[4], t[1], t[2], A.subtract)
+    num(V.tensor_scalar, t[5], t[0], 4.0, None, A.mult)
+    done()
+    num(V.tensor_scalar, t[6], t[4], 1, 1, A.arith_shift_right, A.bitwise_and)
+    num(V.tensor_scalar, t[7], t[4], 1, None, A.bitwise_and)
+    num(V.tensor_tensor, t[8], t[5], t[3], A.add)
+    done()
+    num(V.tensor_scalar, t[1], t[6], 512.0, None, A.mult)
+    num(V.tensor_scalar, t[2], t[7], 2.0, None, A.mult)
+    done()
+    num(V.tensor_tensor, t[9], t[1], t[2], A.add)
+    done()
+    num(V.tensor_tensor, t[0], t[9], t[8], A.add)
+    done()
+    V.tensor_copy(T.off2[:], t[0]).then_inc(S["off2r"], 1)
 
     E.wait_ge(S["vqr"], 1)
-    E.wait_ge(S["rl%d" % (N - 2)], 4)
-    E.wait_ge(S["rl%d" % (N - 1)], 4)
-    for m, a in enumerate(order):
-        if a == rank:
-            E.wait_ge(S["q2_%d" % own], 1)
-            q, sc = T.hq, T.hs
-        else:
-            E.wait_ge(S["in2_%d" % a], 2 * len(near))
-            q, sc = T.bq, T.bs
-        z = T.ps[:, 512 * m:512 * m + B]
-        E.matmul_mx(z, T.vq[:], T.vs[:], q[:, blk(a)], sc[:, blk(a)], True, True).then_inc(S["fm%d" % m], 1)
-        if m % 2 == 0:
-            g.scalar.wait_ge(S["fm%d" % m], 1)
-            g.scalar.activation(T.yv[:, blk(a)], z, F.Copy).then_inc(S["fc"], 1)
-        else:
-            V.wait_ge(S["fm%d" % m], 1)
-            V.tensor_copy(T.yv[:, blk(a)], z).then_inc(S["fc"], 1)
+    E.wait_ge(S["rl6"], 4)
+    E.wait_ge(S["rl7"], 4)
+    m = [0]
+
+    def product(bank, q, sc, lo, w, copies):
+        sem = S["fm%d" % m[0]]
+        m[0] += 1
+        E.matmul_mx(T.ps[:, 512 * bank:512 * bank + w], T.vq[:], T.vs[:], q[:, lo:lo + w], sc[:, lo:lo + w],
+                    True, True).then_inc(sem, 1)
+        for on, a, b, to, fin in copies:
+            z, y = T.ps[:, 512 * bank + a:512 * bank + a + b], T.yv[:, to:to + b]
+            if on == "V":
+                V.wait_ge(sem, 1)
+                V.tensor_copy(y, z).then_inc(S[fin], 1)
+            else:
+                C.wait_ge(sem, 1)
+                C.activation(y, z, F.Copy).then_inc(S[fin], 1)
+
+    for f in range(2):
+        hq, hs, bq, bs = T["hq%d" % f], T["hs%d" % f], T["bq%d" % f], T["bs%d" % f]
+        y0 = HA * f
+        E.wait_ge(S["q2%d_%d" % (f, G - 1)], 1)
+        if f:
+            E.wait_ge(S["fcs"], 1)
+        product(0, hq, hs, B * me, B, [("V", HB * (rank % 2), HB, y0 + HB * rank, "fc" if f else "fcs")])
+        for d in range(3):
+            for a in groups[in_order[d]]:
+                E.wait_ge(S["in2%d_%d" % (f, a)], n if d < 2 else 2 * n)
+            if d == 2:
+                E.wait_ge(S["in2%d_%d" % (f, sib)], 2 * len(near))
+            yd = y0 + B * in_order[d]
+            bank = 4 * f + d + (0 if f else 1)
+            on = "CVC"[d]
+            if d < 2:
+                product(bank, bq, bs, B * d, B, [(on, 0, B, yd, "fc")])
+            elif f == 0:
+                product(bank, bq, bs, B * d, B + HB, [(on, 0, B, yd, "fc"), (on, B, HB, y0 + HB * sib, "fc")])
+            else:
+                product(bank, bq, bs, B * d, B, [("C", 0, B, yd, "fc")])
+                product(bank + 1, bq, bs, B * d + HB, B, [("V", HB, HB, y0 + HB * sib, "fc")])
     H = TOK // 2
-    g.scalar.wait_ge(S["off2r"], 1)
-    g.scalar.wait_ge(S["fc"], N)
-    g.scalar.activation(T.yt[:, 0:H], T.yv[:].indirect(T.off2[:, 0:H // 16]), F.Copy).then_inc(S["yv0"], 1)
-    V.wait_ge(S["off2r"], 1)
-    V.wait_ge(S["fc"], N)
+    for q in (C, V):
+        q.wait_ge(S["off2r"], 1)
+        q.wait_ge(S["fcs"], 1)
+        q.wait_ge(S["fc"], 9)
+    C.activation(T.yt[:, 0:H], T.yv[:].indirect(T.off2[:, 0:H // 16]), F.Copy).then_inc(S["yv0"], 1)
     V.tensor_copy(T.yt[:, H:TOK], T.yv[:].indirect(T.off2[:, H // 16:TOK // 16])).then_inc(S["yv1"], 1)
-    g.scalar.wait_ge(S["yv0"], 1)
-    g.scalar.dma_start(T.y[:, 0:H], T.yt[:, 0:H]).then_inc(S["st0"], 16)
+    C.wait_ge(S["yv0"], 1)
+    C.dma_start(T.y[:, 0:H], T.yt[:, 0:H]).then_inc(S["st0"], 16)
     g.sync.wait_ge(S["yv1"], 1)
     g.sync.dma_start(T.y[:, H:TOK], T.yt[:, H:TOK]).then_inc(S["st1"], 16)
-    g.scalar.wait_ge(S["st0"], 16)
+    C.wait_ge(S["st0"], 16)
     g.sync.wait_ge(S["st1"], 16)
-    g.wait_ge(S["ls"], 2 * ((G - 1) * 2 * len(far) + 2 * len(near)))
+    g.wait_ge(S["ls"], 12 * n + 2 * len(near) + (2 * len(far) + 4 * len(near)) + (4 * len(far) + 2 * len(near)))

from concourse.bass import DstId, RemoteDMATransfer
from concourse.mybir import AluOpType, ActivationFunctionType, dt

N, TOK, TR = 8, 512, 16
B = N * TR
ALL = N * B
HB = B // 2
HA = ALL // 2

SCRATCH = {
    "trib": ("sbuf", [128, ALL // 16], "int32"),
    "off1": ("sbuf", [128, ALL // 16], "uint16"),
    "pltb": ("sbuf", [128, TOK // 16], "int32"),
    "off2": ("sbuf", [128, TOK // 16], "uint16"),
    "xb": ("sbuf", [128, 4 * TOK], "bfloat16"),
    "wb": ("sbuf", [128, 2048], "bfloat16"),
    "vb": ("sbuf", [128, 512], "bfloat16"),
    "xg": ("sbuf", [128, 4 * ALL], "bfloat16"),
    "wq": ("sbuf", [128, 512], "float8_e4m3fn_x4"),
    "ws": ("sbuf", [128, 512], "uint8"),
    "vq": ("sbuf", [128, 128], "float8_e4m3fn_x4"),
    "vs": ("sbuf", [128, 128], "uint8"),
    "xq": ("sbuf", [128, ALL], "float8_e4m3fn_x4"),
    "xs": ("sbuf", [128, ALL], "uint8"),
    "aq": ("sbuf", [128, ALL], "float8_e4m3fn_x4"),
    "as_": ("sbuf", [128, ALL], "uint8"),
    "rq": ("sbuf", [128, B], "float8_e4m3fn_x4"),
    "rs": ("sbuf", [128, B], "uint8"),
    "yv": ("sbuf", [128, ALL], "float32"),
    "yt": ("sbuf", [128, TOK], "float32"),
    "ps": ("psum", [128, 4096], "float32"),
}
for _f in range(2):
    SCRATCH["h%d" % _f] = ("sbuf", [128, 4 * HA], "bfloat16")
    SCRATCH["hq%d" % _f] = ("sbuf", [128, HA], "float8_e4m3fn_x4")
    SCRATCH["hs%d" % _f] = ("sbuf", [128, HA], "uint8")
    SCRATCH["bq%d" % _f] = ("sbuf", [128, 7 * HB], "float8_e4m3fn_x4")
    SCRATCH["bs%d" % _f] = ("sbuf", [128, 7 * HB], "uint8")
for _f in range(10):
    SCRATCH["n%d" % _f] = ("sbuf", [128, TOK // 16], "int32")
SEMAPHORES = (["ld_tri", "ld_x", "ld_w", "ld_v", "ld_plt", "off1r", "off2r", "wqr", "vqr", "pt",
               "ls", "fc", "fcs", "yv0", "yv1", "st0", "st1", "viaq", "vias"]
              + ["gx%d" % p for p in range(4)] + ["q1_%d" % p for p in range(4)]
              + ["q2%d_%d" % (f, p) for p in range(4) for f in range(2)]
              + ["in1_%d" % r for r in range(N)] + ["in2%d_%d" % (f, r) for r in range(N) for f in range(2)]
              + ["ma%d" % k for k in range(N)] + ["mb%d" % k for k in range(N)] + ["rl%d" % k for k in range(N)]
              + ["fm%d" % k for k in range(9)])


def bits(engines):
    return sum(1 << e for e in engines)


def via(r, T, topo):
    c = T.cores[r]
    free = [o for o in topo.cores_of(c) if topo.die(o) != topo.die(c) and T.rank_of(o) is None
            and all(topo.may_write(o, d) for d in T.cores if topo.chip(d) != topo.chip(c))]
    return free[[d for d in T.cores if topo.chip(d) == topo.chip(c)].index(c)]


def rank_program(g, core, T, topo):
    rank = T.rank_of(core)
    hands_on = rank is None
    if hands_on:
        served = [r for r in range(N) if via(r, T, topo) == core]
        if not served:
            return
        rank = served[0]
    S = T.sem
    A = AluOpType
    F = ActivationFunctionType
    V, E, C = g.vector, g.tensor, g.scalar
    chips = []
    for c in T.cores:
        if topo.chip(c) not in chips:
            chips.append(topo.chip(c))
    groups = [[r for r in range(N) if topo.chip(T.cores[r]) == c] for c in chips]
    me = chips.index(topo.chip(core))
    G = len(groups)
    out_order = [(me + d) % G for d in range(1, G)]
    in_order = [(me - d) % G for d in range(1, G)]
    sib = [r for r in groups[me] if r != rank][0]
    PC = 2 * B
    far = topo.engines(core, T.cores[groups[out_order[0]][0]])
    near = [e for e in topo.engines(core, T.cores[sib]) if e not in far][:len(far) // 2]
    n = len(far) // 2

    def share(ranks):
        k = len(far) // len(ranks)
        return [(r, far[k * i:k * (i + 1)]) for i, r in enumerate(ranks)]

    def slot(b, a):
        d = (b // 2 - a // 2) % G
        return 6 if d == 0 else 2 * (d - 1) + a % 2

    def views(src, dst, lo, to, w, code):
        a, b = src[:, lo:lo + w], dst[:, to:to + w]
        return (a.bitcast(dt.uint8), b.bitcast(dt.uint8)) if code else (a, b)

    def send(dsts, src, dst, place, sem, code):
        out = []
        for r, eng in dsts:
            rid, pid, _ = topo.addr(T.cores[r])
            a, b = views(src, dst, *place(r), code)
            out.append(RemoteDMATransfer(dst_ids=[DstId(rid=rid, pnc=pid)], dma_engine_mask=bits(eng),
                                         remote_sem=S["%s_%d" % (sem, rank)], src=a, dst=b))
        g.remote_dma_fused(out, local_sem=S["ls"])

    last = out_order[G - 2]
    if hands_on:
        def place_on(r):
            return HB * groups[last].index(r), HB * slot(r, rank), HB

        g.wait_ge(S["viaq"], len(near))
        send(share(groups[last]), T.rq, T.bq0, place_on, "in20", True)
        g.wait_ge(S["vias"], len(near))
        send(share(groups[last]), T.rs, T.bs0, place_on, "in20", False)
        g.wait_ge(S["ls"], 2 * len(far))
        return

    for k in range(8):
        q = g.sync if k < 3 else C
        q.dma_start(T.trib[16 * k:16 * k + 16, :], T.tri[:]).then_inc(S["ld_tri"], 16)
    g.sync.dma_start(T.xb[:], T.x[:]).then_inc(S["ld_x"], 16)
    g.sync.wait_ge(S["ld_x"], 16)
    g.sync.dma_start(T.wb[:], T.w[:]).then_inc(S["ld_w"], 16)
    g.sync.dma_start(T.vb[:], T.vv[:]).then_inc(S["ld_v"], 16)
    for k in range(8):
        g.sync.dma_start(T.pltb[16 * k:16 * k + 16, :], T.plt[:]).then_inc(S["ld_plt"], 16)

    V.wait_ge(S["ld_tri"], 128)
    V.tensor_scalar(T.off1[:], T.trib[:], 4.0, 0.0, A.mult, A.max).then_inc(S["off1r"], 1)
    V.wait_ge(S["off1r"], 1)
    V.wait_ge(S["ld_x"], 16)
    C.wait_ge(S["off1r"], 1)
    C.wait_ge(S["ld_x"], 16)

    def place1(r):
        return B * r, B * rank, B

    for p, gi in enumerate([out_order[0], me, out_order[1], out_order[2]]):
        c0 = PC * gi
        off = T.off1[:, c0 // 16:(c0 + PC) // 16]
        ns = 3 if gi == me else 2
        for t in range(4):
            o = T.xg[:, 4 * c0 + t:4 * (c0 + PC):4]
            i = T.xb[:, t:4 * TOK].indirect(off)
            if t < ns:
                C.activation(o, i, F.Copy).then_inc(S["gx%d" % p], 1)
            else:
                V.tensor_copy(o, i).then_inc(S["gx%d" % p], 1)
        V.wait_ge(S["gx%d" % p], 4)
        V.quantize_mx(T.xq[:, c0:c0 + PC], T.xs[:, c0:c0 + PC], T.xg[:, 4 * c0:4 * (c0 + PC)]).then_inc(S["q1_%d" % p], 1)
        if gi == me:
            continue
        if p == 2:
            g.wait_ge(S["q1_1"], 1)
        g.wait_ge(S["q1_%d" % p], 1)
        dst = share(groups[gi]) + ([(sib, near)] if p == 2 else [])
        send(dst, T.xq, T.aq, place1, "in1", True)
        send(dst, T.xs, T.as_, place1, "in1", False)

    V.wait_ge(S["ld_w"], 16)
    V.quantize_mx(T.wq[:], T.ws[:], T.wb[:]).then_inc(S["wqr"], 1)
    V.wait_ge(S["ld_v"], 16)
    V.quantize_mx(T.vq[:], T.vs[:], T.vb[:]).then_inc(S["vqr"], 1)

    E.wait_ge(S["wqr"], 1)
    halves = [[rank] + groups[in_order[0]] + [sib], groups[in_order[1]] + groups[in_order[2]]]
    k = 0
    for f, half in enumerate(halves):
        h, hq, hs = T["h%d" % f], T["hq%d" % f], T["hs%d" % f]
        for s in half:
            if s == rank:
                E.wait_ge(S["q1_1"], 1)
                q, sc = T.xq, T.xs
            else:
                E.wait_ge(S["in1_%d" % s], 2 * n)
                q, sc = T.aq, T.as_
            if k >= 2:
                E.wait_ge(S["rl%d" % (k - 2)], 4)
            base = 2048 * (k % 2)
            for i in (0, 2, 1, 3):
                sem = S[("ma%d" if i < 2 else "mb%d") % k]
                E.matmul_mx(T.ps[:, base + 512 * i:base + 512 * i + B], T.wq[:, 128 * i:128 * i + 128],
                            T.ws[:, 128 * i:128 * i + 128], q[:, B * s:B * s + B], sc[:, B * s:B * s + B],
                            True, True).then_inc(sem, 1)
            C.wait_ge(S["ma%d" % k], 2)
            V.wait_ge(S["mb%d" % k], 2)
            place = 2 * ((me - s // 2) % G % 2) + s % 2
            for i in range(4):
                o = h[:, 4 * place + i:4 * HA:16]
                z = T.ps[:, base + 512 * i:base + 512 * i + B]
                if i < 2:
                    C.activation(o, z, F.Relu, scale=0.043).then_inc(S["rl%d" % k], 1)
                else:
                    V.tensor_scalar(o, z, 0.0, 0.043, A.max, A.mult).then_inc(S["rl%d" % k], 1)
            k += 1
        for j in range(k - 4, k):
            V.wait_ge(S["rl%d" % j], 4)
        by = out_order + [me]
        for p in ((2, 0, 1, 3) if f == 0 else (0, 1, 2, 3)):
            c0 = B * by[p]
            V.quantize_mx(hq[:, c0:c0 + B], hs[:, c0:c0 + B], h[:, 4 * c0:4 * (c0 + B)]).then_inc(S["q2%d_%d" % (f, p)], 1)

        def place2(r):
            return HB * r, HB * slot(r, rank), HB

        if f == 0:
            g.wait_ge(S["q20_2"], 1)
            rid, pid, _ = topo.addr(via(rank, T, topo))
            for src, dst, code, sem in ((hq, T.rq, True, "viaq"), (hs, T.rs, False, "vias")):
                a, b = views(src, dst, B * last, 0, B, code)
                g.remote_dma_fused([RemoteDMATransfer(dst_ids=[DstId(rid=rid, pnc=pid)], dma_engine_mask=bits(near),
                                                      remote_sem=S[sem], src=a, dst=b)], local_sem=S["ls"])
            calls = ((0, 1, 3),)
        else:
            calls = ((0, 1), (2, 3))
        for ps in calls:
            for p in ps:
                g.wait_ge(S["q2%d_%d" % (f, p)], 1)
            dst = share([r for p in ps if p < G - 1 for r in groups[by[p]]]) + ([(sib, near)] if 3 in ps else [])
            send(dst, hq, T["bq%d" % f], place2, "in2%d" % f, True)
            send(dst, hs, T["bs%d" % f], place2, "in2%d" % f, False)

    cnt = [0]

    def num(call, *args):
        call(*args).then_inc(S["pt"], 1)
        cnt[0] += 1

    def done():
        V.wait_ge(S["pt"], cnt[0])

    t = [T["n%d" % i][:] for i in range(10)]
    V.wait_ge(S["ld_plt"], 128)
    num(V.tensor_scalar, t[0], T.pltb[:], 127, None, A.bitwise_and)
    num(V.tensor_scalar, t[1], T.pltb[:], 5, 3, A.logical_shift_right, A.bitwise_and)
    num(V.tensor_scalar, t[2], T.pltb[:], 8, None, A.logical_shift_right)
    num(V.tensor_scalar, t[3], T.pltb[:], 7, 1, A.logical_shift_right, A.bitwise_and)
    done()
    num(V.tensor_tensor, t[4], t[1], t[2], A.subtract)
    num(V.tensor_scalar, t[5], t[0], 4.0, None, A.mult)
    done()
    num(V.tensor_scalar, t[6], t[4], 1, 1, A.arith_shift_right, A.bitwise_and)
    num(V.tensor_scalar, t[7], t[4], 1, None, A.bitwise_and)
    num(V.tensor_tensor, t[8], t[5], t[3], A.add)
    done()
    num(V.tensor_scalar, t[1], t[6], 512.0, None, A.mult)
    num(V.tensor_scalar, t[2], t[7], 2.0, None, A.mult)
    done()
    num(V.tensor_tensor, t[9], t[1], t[2], A.add)
    done()
    num(V.tensor_tensor, t[0], t[9], t[8], A.add)
    done()
    V.tensor_copy(T.off2[:], t[0]).then_inc(S["off2r"], 1)

    E.wait_ge(S["vqr"], 1)
    E.wait_ge(S["rl6"], 4)
    E.wait_ge(S["rl7"], 4)
    m = [0]

    def product(bank, q, sc, lo, w, copies):
        sem = S["fm%d" % m[0]]
        m[0] += 1
        E.matmul_mx(T.ps[:, 512 * bank:512 * bank + w], T.vq[:], T.vs[:], q[:, lo:lo + w], sc[:, lo:lo + w],
                    True, True).then_inc(sem, 1)
        for on, a, b, to, fin in copies:
            z, y = T.ps[:, 512 * bank + a:512 * bank + a + b], T.yv[:, to:to + b]
            if on == "V":
                V.wait_ge(sem, 1)
                V.tensor_copy(y, z).then_inc(S[fin], 1)
            else:
                C.wait_ge(sem, 1)
                C.activation(y, z, F.Copy).then_inc(S[fin], 1)

    for f in range(2):
        hq, hs, bq, bs = T["hq%d" % f], T["hs%d" % f], T["bq%d" % f], T["bs%d" % f]
        y0 = HA * f
        E.wait_ge(S["q2%d_%d" % (f, G - 1)], 1)
        if f:
            E.wait_ge(S["fcs"], 1)
        product(0, hq, hs, B * me, B, [("V", HB * (rank % 2), HB, y0 + HB * rank, "fc" if f else "fcs")])
        for d in range(3):
            for a in groups[in_order[d]]:
                E.wait_ge(S["in2%d_%d" % (f, a)], n if d < 2 else 2 * n)
            if d == 2:
                E.wait_ge(S["in2%d_%d" % (f, sib)], 2 * len(near))
            yd = y0 + B * in_order[d]
            bank = 4 * f + d + (0 if f else 1)
            on = "CVC"[d]
            if d < 2:
                product(bank, bq, bs, B * d, B, [(on, 0, B, yd, "fc")])
            elif f == 0:
                product(bank, bq, bs, B * d, B + HB, [(on, 0, B, yd, "fc"), (on, B, HB, y0 + HB * sib, "fc")])
            else:
                product(bank, bq, bs, B * d, B, [("C", 0, B, yd, "fc")])
                product(bank + 1, bq, bs, B * d + HB, B, [("V", HB, HB, y0 + HB * sib, "fc")])
    H = TOK // 2
    for q in (C, V):
        q.wait_ge(S["off2r"], 1)
        q.wait_ge(S["fcs"], 1)
        q.wait_ge(S["fc"], 9)
    C.activation(T.yt[:, 0:H], T.yv[:].indirect(T.off2[:, 0:H // 16]), F.Copy).then_inc(S["yv0"], 1)
    V.tensor_copy(T.yt[:, H:TOK], T.yv[:].indirect(T.off2[:, H // 16:TOK // 16])).then_inc(S["yv1"], 1)
    C.wait_ge(S["yv0"], 1)
    C.dma_start(T.y[:, 0:H], T.yt[:, 0:H]).then_inc(S["st0"], 16)
    g.sync.wait_ge(S["yv1"], 1)
    g.sync.dma_start(T.y[:, H:TOK], T.yt[:, H:TOK]).then_inc(S["st1"], 16)
    C.wait_ge(S["st0"], 16)
    g.sync.wait_ge(S["st1"], 16)
    g.wait_ge(S["ls"], 12 * n + 2 * len(near) + (2 * len(far) + 4 * len(near)) + (4 * len(far) + 2 * len(near)))
